import numpy as np
import ml_dtypes


def mxq(x, axis, fmt="e4m3"):
    dtype, down = {"e4m3": (ml_dtypes.float8_e4m3fn, 7), "e5m2": (ml_dtypes.float8_e5m2, 14)}[fmt]
    v = np.moveaxis(np.asarray(x, np.float32).astype(ml_dtypes.bfloat16).astype(np.float64), axis, -1)
    blocks = v.reshape(v.shape[:-1] + (-1, 32))
    amax = np.abs(blocks).max(-1, keepdims=True)
    byte = np.maximum(np.where(amax > 0, np.frexp(amax)[1] - 1 + 127, 0) - down, 1)
    scale = np.exp2(byte - 127.0)
    codes = (blocks / scale).astype(np.float32).astype(dtype).astype(np.float64)
    return np.moveaxis((codes * scale).reshape(v.shape), -1, axis)


WIDE = False


def mx_kscale(k):
    if not WIDE:
        return np.ones(k)
    levels = np.array([10, -10, 5, -5, 0])
    if k % 512:
        return np.exp2(np.random.permutation(np.resize(levels, k // 32))).repeat(32)
    a = np.empty((k // 512, 16))
    for p in range(k // 512):
        a[p, :8] = np.random.permutation(np.resize(levels, 8))
        for g in range(8):
            far = levels[np.abs(levels - a[p, g]) >= 10]
            a[p, g + 8] = far[np.random.randint(len(far))]
    return np.exp2(a.ravel()).repeat(32)


def f64(x):
    return np.asarray(x).astype(np.float64)


def striped(idx):
    return np.tile(idx.reshape(-1, 16).T, (8, 1)).astype(np.uint16)


def unstriped(offs):
    return offs[:16].T.reshape(-1).astype(np.int64)


def pack_weight(w):
    k, n = w.shape
    w = f64(np.asarray(w, np.float32).astype(ml_dtypes.bfloat16)).reshape(k // 32, 32, n)
    amax = np.abs(w).max(1)
    byte = np.clip(np.where(amax > 0, np.frexp(amax)[1] - 1 + 127 - 7, 1), 1, 254)
    scaled = (w * np.exp2(127.0 - byte)[:, None, :]).reshape(k, n).astype(np.float32)
    words = np.ascontiguousarray(scaled.reshape(k // 512, 128, 4, n).transpose(0, 1, 3, 2)).astype(ml_dtypes.float8_e4m3fn).view(np.uint8)
    return words, np.ascontiguousarray(byte.astype(np.uint8).reshape(k // 512, 16, n))


def unpack_weight(words, scales):
    g, p, n, _ = words.shape
    vals = np.ascontiguousarray(words).view(ml_dtypes.float8_e4m3fn).astype(np.float64) * np.repeat(np.exp2(scales.astype(np.float64) - 127.0), 8, axis=1)[..., None]
    return vals.transpose(0, 1, 3, 2).reshape(g * 512, n)


K, T, S, V, D, R, W = 1024, 2048, 1024, 512, 4, 256, 256


def setup_inputs():
    n = np.random.standard_normal
    s = mx_kscale(K)[:, None]
    packed_xT = pack_weight(n((K, T)) * s)
    return {
        "x_words": packed_xT[0],
        "x_scales": packed_xT[1],
        "hT": (n((K, V)) / np.sqrt(K) / s).astype(np.float32),
        "alpha": (n((V, R))).astype(np.float32),
        "beta": (n((V, R))).astype(np.float32),
        "prior": (n((V, W))).astype(np.float32),
        "offs": striped(np.random.permutation(T)[:S]),
        "st": striped(np.random.permutation(np.concatenate([np.arange(R), np.random.randint(0, R, S - R)]))),
        "en": striped(np.random.permutation(np.concatenate([np.arange(R), np.random.randint(0, R, S - R)]))),
        "one": striped(np.random.permutation(W)),
        "zero": striped(np.random.permutation(W)),
    }


def reference(x_words, x_scales, hT, alpha, beta, prior, offs, st, en, one, zero):
    hTq = mxq(f64(hT), 0, "e4m3")
    xq = unpack_weight(x_words, x_scales)[:, unstriped(offs)]
    y = hTq.T @ xq
    mt = y + f64(alpha)[:, unstriped(st)] + f64(beta)[:, unstriped(en)]
    ex = np.exp(0.5 * mt)
    mg = np.log(ex.reshape(len(ex), -1, D).sum(axis=2))
    return 0.7 * (mg[:, unstriped(one)] - mg[:, unstriped(zero)] - f64(prior))

@@ -1,0 +1,262 @@
+from contextlib import ExitStack
+
+import concourse.mybir as mybir
+from concourse.masks import make_identity
+
+K, T, S, V, D, R, W = 1024, 2048, 1024, 512, 4, 256, 256
+FLOPS = 2 * K * S * V
+
+F32 = mybir.dt.float32
+BF16 = mybir.dt.bfloat16
+I32 = mybir.dt.int32
+U32 = mybir.dt.uint32
+U16 = mybir.dt.uint16
+U8 = mybir.dt.uint8
+FP8X4 = mybir.dt.float8_e4m3fn_x4
+ACT = mybir.ActivationFunctionType
+ALU = mybir.AluOpType
+
+P = 128
+PACK = 4
+K_PASS = P * PACK
+PASSES = K // K_PASS
+TILES = V // P
+HALF = 512
+HALVES = S // HALF
+COLS = HALF // 16
+CHUNK = 256
+ALPHA_WINDOW = 2048
+BETA_WINDOW = HALF + 16
+MG_WINDOW = 512
+
+
+def tile_picked_ybcjr_log_p_kernel(
+    tc, x_words, x_scales, hT, alpha, beta, prior, offs, st, en, one, zero, out
+):
+    nc = tc.nc
+    with ExitStack() as ctx:
+        lists = ctx.enter_context(tc.tile_pool(name="lists", bufs=1))
+        keep = ctx.enter_context(tc.tile_pool(name="keep", bufs=1))
+        psum = ctx.enter_context(tc.psum_pool(name="psum", bufs=1))
+
+        def load_list(name, src):
+            tile = lists.tile(list(src.shape), U16, name=name)
+            nc.sync.dma_start(tile[:], src)
+            return tile
+
+        def rows(tt):
+            return slice(tt * P, (tt + 1) * P)
+
+        def piece(h):
+            return slice(h * COLS, (h + 1) * COLS)
+
+        warm = keep.tile([P, 2], F32, name="warm")
+        nc.vector.memset(warm[:, 0:1], 0.0)
+        nc.scalar.activation(warm[:, 1:2], warm[:, 0:1], ACT.Exp)
+        scale_table = keep.tile([P, T], U8, name="scale_table", align_bytes=64)
+        nc.vector.memset(scale_table[:].bitcast(I32), 0)
+        alpha_win = [keep.tile([P, ALPHA_WINDOW], F32, name="alpha_win%d" % tt) for tt in range(TILES)]
+        beta_raw = [keep.tile([P, R], F32, name="beta_raw%d" % tt) for tt in range(TILES)]
+        beta_win = [keep.tile([P, BETA_WINDOW], F32, name="beta_win%d" % tt) for tt in range(TILES)]
+        mg_win = [keep.tile([P, MG_WINDOW], F32, name="mg_win%d" % tt) for tt in range(TILES)]
+        ident = keep.tile([P, P], F32, name="ident")
+        make_identity(nc, ident[:])
+
+        word_table = [keep.tile([P, T], I32, name="word_table%d" % o) for o in range(PASSES)]
+        h_raw = {}
+
+        def load_alpha(tt):
+            nc.sync.dma_start(alpha_win[tt][:, :R], alpha[rows(tt), :])
+
+        def load_beta(tt):
+            nc.sync.dma_start(beta_raw[tt][:], beta[rows(tt), :])
+
+        def load_words(o):
+            nc.sync.dma_start(word_table[o][:], x_words[o].rearrange("p n t -> p (n t)").bitcast(I32))
+
+        def load_scales():
+            for q in range(4):
+                nc.sync.dma_start(
+                    scale_table[32 * q : 32 * q + 4 * PASSES, :].bitcast(I32),
+                    x_scales[:, 4 * q : 4 * q + 4, :].bitcast(I32),
+                )
+
+        def load_h(c, o):
+            h_raw[c, o] = keep.tile([P, PACK, CHUNK], F32, name="h_raw%d_%d" % (c, o))
+            src = hT[o * K_PASS : (o + 1) * K_PASS, c * CHUNK : (c + 1) * CHUNK]
+            nc.sync.dma_start(h_raw[c, o][:], src.rearrange("(p j) w -> p j w", j=PACK))
+
+        st_l = load_list("st_l", st)
+        load_alpha(0)
+        offs_l = load_list("offs_l", offs)
+        load_words(0)
+        load_scales()
+        load_alpha(1)
+        load_beta(0)
+        en_l = load_list("en_l", en)
+        load_h(0, 0)
+        load_words(1)
+        load_h(0, 1)
+        load_alpha(2)
+        load_beta(1)
+        load_h(1, 0)
+        load_h(1, 1)
+        load_alpha(3)
+        load_beta(2)
+        load_beta(3)
+        one_l = load_list("one_l", one)
+        zero_l = load_list("zero_l", zero)
+        prior_sb = keep.tile([P, TILES, W], F32, name="prior_sb")
+        nc.sync.dma_start(prior_sb[:], prior.rearrange("(n p) w -> p n w", p=P))
+
+        ea, ab, words, scales, h_bf, h_codes, h_scales, ey, q2, sums = {}, {}, {}, {}, {}, {}, {}, {}, {}, {}
+
+        def exp_beta(tt):
+            nc.scalar.activation(beta_win[tt][:, :R], beta_raw[tt][:], ACT.Exp, scale=0.5)
+
+        def gather_alpha(tt, h):
+            ea[tt, h] = keep.tile([P, HALF], F32, name="ea%d_%d" % (tt, h))
+            nc.scalar.activation(ea[tt, h][:], alpha_win[tt][:].indirect(st_l[:, piece(h)]), ACT.Exp, scale=0.5)
+
+        def gather_beta(tt, h):
+            ab[tt, h] = keep.tile([P, HALF], F32, name="ab%d_%d" % (tt, h))
+            nc.vector.tensor_tensor(ab[tt, h][:], beta_win[tt][:].indirect(en_l[:, piece(h)]), ea[tt, h][:], ALU.mult)
+
+        def gather_words(o, h):
+            words[o, h] = keep.tile([P, HALF], U32, name="words%d_%d" % (o, h), align_bytes=64)
+            nc.vector.tensor_copy(words[o, h][:], word_table[o][:].bitcast(U32).indirect(offs_l[:, piece(h)]))
+
+        def gather_scales(h):
+            scales[h] = keep.tile([P, HALF], U8, name="scales%d" % h, align_bytes=64)
+            nc.vector.tensor_copy(scales[h][:], scale_table[:].indirect(offs_l[:, piece(h)]))
+
+        def weave(c, o):
+            h_bf[c, o] = keep.tile([P, CHUNK, PACK], BF16, name="h_bf%d_%d" % (c, o), align_bytes=64)
+            nc.scalar.copy(h_bf[c, o][:], h_raw[c, o][:].rearrange("p j w -> p w j"))
+
+        def quantize(c, o):
+            h_codes[c, o] = keep.tile([P, CHUNK], U32, name="h_codes%d_%d" % (c, o), align_bytes=64)
+            h_scales[c, o] = keep.tile([P, CHUNK], U8, name="h_scales%d_%d" % (c, o), align_bytes=64)
+            nc.vector.quantize_mx(
+                out=h_codes[c, o][:].bitcast(FP8X4),
+                scales=h_scales[c, o][:],
+                in_=h_bf[c, o][:].rearrange("p w j -> p (w j)"),
+            )
+
+        def product(tt, h):
+            c, cols = tt // 2, slice((tt % 2) * P, (tt % 2 + 1) * P)
+            y = psum.tile([P, HALF], F32, name="y", tag="bank%d" % ((2 * tt + h) % 4))
+            for o in range(PASSES):
+                nc.tensor.matmul_mx(
+                    out=y[:],
+                    lhsT=h_codes[c, o][:, cols].bitcast(FP8X4),
+                    lhsT_scale=h_scales[c, o][:, cols],
+                    rhs=words[o, h][:].bitcast(FP8X4),
+                    rhs_scale=scales[h][4 * o : P, :],
+                    start=(o == 0),
+                    stop=(o == PASSES - 1),
+                )
+            ey[tt, h] = keep.tile([P, 2, HALF // 2], F32, name="ey%d_%d" % (tt, h))
+            nc.scalar.activation(ey[tt, h][:], y[:].rearrange("p (m e) -> p e m", e=2), ACT.Exp, scale=0.5)
+
+        def multiply(tt, h):
+            q2[tt, h] = keep.tile([P, 2, HALF // 2], F32, name="q2%d_%d" % (tt, h))
+            nc.vector.tensor_tensor(
+                q2[tt, h][:].rearrange("p e (b i) -> p b e i", i=4),
+                ab[tt, h][:].rearrange("p (b i e) -> p b e i", i=4, e=2),
+                ey[tt, h][:].rearrange("p e (b i) -> p b e i", i=4),
+                ALU.mult,
+            )
+
+        def add_groups(tt):
+            turned = psum.tile([P, HALVES, P], F32, name="turned", tag="bank%d" % (4 + tt % 2))
+            for h in range(HALVES):
+                for d in range(D):
+                    nc.tensor.matmul(
+                        turned[:, h, :],
+                        lhsT=q2[tt, h][:, d % 2, d // 2 : HALF // 2 : 2],
+                        rhs=ident[:],
+                        is_transpose=True,
+                        start=(d == 0),
+                        stop=(d == D - 1),
+                    )
+            sums[tt] = keep.tile([P, HALVES, P], F32, name="sums%d" % tt)
+            nc.scalar.copy(sums[tt][:], turned[:])
+
+        def log_sums(tt, bank):
+            back = psum.tile([P, W], F32, name="back", tag=bank)
+            for h in range(HALVES):
+                nc.tensor.transpose(back[:, h * P : (h + 1) * P], sums[tt][:, h, :], ident[:])
+            nc.scalar.activation(mg_win[tt][:, :W], back[:], ACT.Ln)
+
+        def finish(tt):
+            low = keep.tile([P, W], F32, name="low%d" % tt)
+            nc.vector.tensor_tensor(low[:], mg_win[tt][:].indirect(zero_l[:]), prior_sb[:, tt, :], ALU.add)
+            diff = keep.tile([P, W], F32, name="diff%d" % tt)
+            nc.vector.tensor_tensor(diff[:], mg_win[tt][:].indirect(one_l[:]), low[:], ALU.subtract)
+            res = keep.tile([P, W], F32, name="res%d" % tt)
+            nc.scalar.activation(res[:], diff[:], ACT.Copy, scale=0.7)
+            nc.scalar.dma_start(out[rows(tt), :], res[:])
+
+        gather_alpha(0, 0)
+        gather_alpha(0, 1)
+        gather_words(0, 0)
+        gather_words(0, 1)
+        gather_alpha(1, 0)
+        exp_beta(0)
+        weave(0, 0)
+        gather_scales(0)
+        gather_beta(0, 0)
+        gather_alpha(1, 1)
+        gather_words(1, 0)
+        quantize(0, 0)
+        weave(0, 1)
+        gather_words(1, 1)
+        quantize(0, 1)
+        exp_beta(1)
+        gather_scales(1)
+        gather_alpha(2, 0)
+        product(0, 0)
+        gather_beta(0, 1)
+        weave(1, 0)
+        gather_beta(1, 0)
+        weave(1, 1)
+        product(0, 1)
+        gather_beta(1, 1)
+        quantize(1, 0)
+        multiply(0, 0)
+        quantize(1, 1)
+        product(1, 0)
+        gather_alpha(2, 1)
+        exp_beta(2)
+        multiply(0, 1)
+        product(1, 1)
+        gather_beta(2, 0)
+        gather_alpha(3, 0)
+        multiply(1, 0)
+        gather_beta(2, 1)
+        exp_beta(3)
+        gather_alpha(3, 1)
+        multiply(1, 1)
+        product(2, 0)
+        product(2, 1)
+        gather_beta(3, 0)
+        product(3, 0)
+        product(3, 1)
+        add_groups(0)
+        gather_beta(3, 1)
+        add_groups(1)
+        multiply(2, 0)
+        multiply(2, 1)
+        multiply(3, 0)
+        multiply(3, 1)
+        log_sums(0, "bank3")
+        add_groups(2)
+        log_sums(1, "bank2")
+        finish(0)
+        add_groups(3)
+        finish(1)
+        log_sums(2, "bank6")
+        finish(2)
+        log_sums(3, "bank7")
+        finish(3)

@@ -25,6 +25,7 @@ HALF = 512
 HALVES = S // HALF
 COLS = HALF // 16
 CHUNK = 256
+SCALAR_BETA = (1, 2)
 ALPHA_WINDOW = 2048
 BETA_WINDOW = HALF + 16
 MG_WINDOW = 512
@@ -37,6 +38,7 @@ def tile_picked_ybcjr_log_p_kernel(
     with ExitStack() as ctx:
         lists = ctx.enter_context(tc.tile_pool(name="lists", bufs=1))
         keep = ctx.enter_context(tc.tile_pool(name="keep", bufs=1))
+        late = ctx.enter_context(tc.tile_pool(name="late", bufs=1))
         psum = ctx.enter_context(tc.psum_pool(name="psum", bufs=1))
 
         def load_list(name, src):
@@ -50,15 +52,18 @@ def tile_picked_ybcjr_log_p_kernel(
         def piece(h):
             return slice(h * COLS, (h + 1) * COLS)
 
-        warm = keep.tile([P, 2], F32, name="warm")
+        warm = keep.tile([P, 3], F32, name="warm")
         nc.vector.memset(warm[:, 0:1], 0.0)
         nc.scalar.activation(warm[:, 1:2], warm[:, 0:1], ACT.Exp)
         scale_table = keep.tile([P, T], U8, name="scale_table", align_bytes=64)
         nc.vector.memset(scale_table[:].bitcast(I32), 0)
-        alpha_win = [keep.tile([P, ALPHA_WINDOW], F32, name="alpha_win%d" % tt) for tt in range(TILES)]
-        beta_raw = [keep.tile([P, R], F32, name="beta_raw%d" % tt) for tt in range(TILES)]
+        alpha_win = [keep.tile([P, ALPHA_WINDOW], F32, name="alpha_win%d" % tt) for tt in range(TILES - 1)]
+        alpha_win.append(late.tile([P, ALPHA_WINDOW], F32, name="alpha_win3", offset=0))
+        beta_raw = [
+            keep.tile([P, ALPHA_WINDOW if tt in SCALAR_BETA else R], F32, name="beta_raw%d" % tt) for tt in range(TILES)
+        ]
         beta_win = [keep.tile([P, BETA_WINDOW], F32, name="beta_win%d" % tt) for tt in range(TILES)]
-        mg_win = [keep.tile([P, MG_WINDOW], F32, name="mg_win%d" % tt) for tt in range(TILES)]
+        mg_win = {}
         ident = keep.tile([P, P], F32, name="ident")
         make_identity(nc, ident[:])
 
@@ -69,7 +74,7 @@ def tile_picked_ybcjr_log_p_kernel(
             nc.sync.dma_start(alpha_win[tt][:, :R], alpha[rows(tt), :])
 
         def load_beta(tt):
-            nc.sync.dma_start(beta_raw[tt][:], beta[rows(tt), :])
+            nc.sync.dma_start(beta_raw[tt][:, :R], beta[rows(tt), :])
 
         def load_words(o):
             nc.sync.dma_start(word_table[o][:], x_words[o].rearrange("p n t -> p (n t)").bitcast(I32))
@@ -88,39 +93,50 @@ def tile_picked_ybcjr_log_p_kernel(
 
         st_l = load_list("st_l", st)
         load_alpha(0)
+        load_h(0, 0)
+        load_beta(0)
+        en_l = load_list("en_l", en)
+        load_alpha(1)
+        load_beta(1)
+        load_h(0, 1)
         offs_l = load_list("offs_l", offs)
         load_words(0)
         load_scales()
-        load_alpha(1)
-        load_beta(0)
-        en_l = load_list("en_l", en)
-        load_h(0, 0)
-        load_words(1)
-        load_h(0, 1)
         load_alpha(2)
-        load_beta(1)
+        load_beta(2)
+        load_alpha(3)
+        load_words(1)
         load_h(1, 0)
         load_h(1, 1)
-        load_alpha(3)
-        load_beta(2)
         load_beta(3)
         one_l = load_list("one_l", one)
         zero_l = load_list("zero_l", zero)
         prior_sb = keep.tile([P, TILES, W], F32, name="prior_sb")
         nc.sync.dma_start(prior_sb[:], prior.rearrange("(n p) w -> p n w", p=P))
 
+        eb, ys, turns, results = {}, {}, {}, []
         ea, ab, words, scales, h_bf, h_codes, h_scales, ey, q2, sums = {}, {}, {}, {}, {}, {}, {}, {}, {}, {}
 
         def exp_beta(tt):
-            nc.scalar.activation(beta_win[tt][:, :R], beta_raw[tt][:], ACT.Exp, scale=0.5)
+            nc.scalar.activation(beta_win[tt][:, :R], beta_raw[tt][:, :R], ACT.Exp, scale=0.5)
 
         def gather_alpha(tt, h):
-            ea[tt, h] = keep.tile([P, HALF], F32, name="ea%d_%d" % (tt, h))
+            tag = "h_codes1_1" if (tt, h) == (3, 1) else "ea%d_%d" % (tt, h)
+            ea[tt, h] = keep.tile([P, HALF], F32, name="ea%d_%d" % (tt, h), tag=tag, align_bytes=64)
             nc.scalar.activation(ea[tt, h][:], alpha_win[tt][:].indirect(st_l[:, piece(h)]), ACT.Exp, scale=0.5)
 
         def gather_beta(tt, h):
-            ab[tt, h] = keep.tile([P, HALF], F32, name="ab%d_%d" % (tt, h))
+            tag = "ab0_1" if (tt, h) == (3, 0) else "ab%d_%d" % (tt, h)
+            ab[tt, h] = keep.tile([P, HALF], F32, name="ab%d_%d" % (tt, h), tag=tag, align_bytes=64)
             nc.vector.tensor_tensor(ab[tt, h][:], beta_win[tt][:].indirect(en_l[:, piece(h)]), ea[tt, h][:], ALU.mult)
+
+        def scalar_beta(tt, h):
+            eb[tt, h] = keep.tile([P, HALF], F32, name="eb%d_%d" % (tt, h))
+            nc.scalar.activation(eb[tt, h][:], beta_raw[tt][:].indirect(en_l[:, piece(h)]), ACT.Exp, scale=0.5)
+
+        def join(tt, h):
+            ab[tt, h] = keep.tile([P, HALF], F32, name="ab%d_%d" % (tt, h))
+            nc.gpsimd.tensor_tensor(ab[tt, h][:], eb[tt, h][:], ea[tt, h][:], ALU.mult)
 
         def gather_words(o, h):
             words[o, h] = keep.tile([P, HALF], U32, name="words%d_%d" % (o, h), align_bytes=64)
@@ -132,7 +148,10 @@ def tile_picked_ybcjr_log_p_kernel(
 
         def weave(c, o):
             h_bf[c, o] = keep.tile([P, CHUNK, PACK], BF16, name="h_bf%d_%d" % (c, o), align_bytes=64)
-            nc.scalar.copy(h_bf[c, o][:], h_raw[c, o][:].rearrange("p j w -> p w j"))
+            nc.vector.tensor_copy(
+                h_bf[c, o][:].rearrange("p (w i) j -> p w j i", i=4),
+                h_raw[c, o][:].rearrange("p j (w i) -> p w j i", i=4),
+            )
 
         def quantize(c, o):
             h_codes[c, o] = keep.tile([P, CHUNK], U32, name="h_codes%d_%d" % (c, o), align_bytes=64)
@@ -144,8 +163,9 @@ def tile_picked_ybcjr_log_p_kernel(
             )
 
         def product(tt, h):
-            c, cols = tt // 2, slice((tt % 2) * P, (tt % 2 + 1) * P)
-            y = psum.tile([P, HALF], F32, name="y", tag="bank%d" % ((2 * tt + h) % 4))
+            c, first = divmod(tt * P, CHUNK)
+            cols = slice(first, first + P)
+            y = psum.tile([P, HALF], F32, name="y", tag="bank%d" % (2 * tt + h))
             for o in range(PASSES):
                 nc.tensor.matmul_mx(
                     out=y[:],
@@ -156,11 +176,16 @@ def tile_picked_ybcjr_log_p_kernel(
                     start=(o == 0),
                     stop=(o == PASSES - 1),
                 )
-            ey[tt, h] = keep.tile([P, 2, HALF // 2], F32, name="ey%d_%d" % (tt, h))
-            nc.scalar.activation(ey[tt, h][:], y[:].rearrange("p (m e) -> p e m", e=2), ACT.Exp, scale=0.5)
+            ys[tt, h] = y
+
+        def exp_y(tt, h):
+            tag = "beta_raw2" if (tt, h) == (0, 0) else "ey%d_%d" % (tt, h)
+            ey[tt, h] = keep.tile([P, 2, HALF // 2], F32, name="ey%d_%d" % (tt, h), tag=tag)
+            nc.scalar.activation(ey[tt, h][:], ys[tt, h][:].rearrange("p (m e) -> p e m", e=2), ACT.Exp, scale=0.5)
 
         def multiply(tt, h):
-            q2[tt, h] = keep.tile([P, 2, HALF // 2], F32, name="q2%d_%d" % (tt, h))
+            tag = "h_bf1_1" if (tt, h) == (0, 0) else "q2%d_%d" % (tt, h)
+            q2[tt, h] = keep.tile([P, 2, HALF // 2], F32, name="q2%d_%d" % (tt, h), tag=tag, align_bytes=64)
             nc.vector.tensor_tensor(
                 q2[tt, h][:].rearrange("p e (b i) -> p b e i", i=4),
                 ab[tt, h][:].rearrange("p (b i e) -> p b e i", i=4, e=2),
@@ -169,7 +194,7 @@ def tile_picked_ybcjr_log_p_kernel(
             )
 
         def add_groups(tt):
-            turned = psum.tile([P, HALVES, P], F32, name="turned", tag="bank%d" % (4 + tt % 2))
+            turned = psum.tile([P, HALVES, P], F32, name="turned", tag="bank%d" % ((tt - 1) % 4))
             for h in range(HALVES):
                 for d in range(D):
                     nc.tensor.matmul(
@@ -180,13 +205,23 @@ def tile_picked_ybcjr_log_p_kernel(
                         start=(d == 0),
                         stop=(d == D - 1),
                     )
-            sums[tt] = keep.tile([P, HALVES, P], F32, name="sums%d" % tt)
-            nc.scalar.copy(sums[tt][:], turned[:])
+            turns[tt] = turned
+
+        def keep_sums(tt):
+            if tt == 0:
+                sums[tt] = keep.tile([P, HALVES, P], F32, name="sums0", tag="words1_1", align_bytes=64)
+            else:
+                sums[tt] = late.tile([P, HALVES, P], F32, name="sums%d" % tt, offset=1024 * (1 + tt))
+            nc.scalar.copy(sums[tt][:], turns[tt][:])
 
         def log_sums(tt, bank):
             back = psum.tile([P, W], F32, name="back", tag=bank)
             for h in range(HALVES):
                 nc.tensor.transpose(back[:, h * P : (h + 1) * P], sums[tt][:, h, :], ident[:])
+            if tt == 0:
+                mg_win[tt] = late.tile([P, MG_WINDOW], F32, name="mg_win0", offset=0)
+            else:
+                mg_win[tt] = keep.tile([P, MG_WINDOW], F32, name="mg_win%d" % tt)
             nc.scalar.activation(mg_win[tt][:, :W], back[:], ACT.Ln)
 
         def finish(tt):
@@ -194,69 +229,85 @@ def tile_picked_ybcjr_log_p_kernel(
             nc.vector.tensor_tensor(low[:], mg_win[tt][:].indirect(zero_l[:]), prior_sb[:, tt, :], ALU.add)
             diff = keep.tile([P, W], F32, name="diff%d" % tt)
             nc.vector.tensor_tensor(diff[:], mg_win[tt][:].indirect(one_l[:]), low[:], ALU.subtract)
-            res = keep.tile([P, W], F32, name="res%d" % tt)
-            nc.scalar.activation(res[:], diff[:], ACT.Copy, scale=0.7)
-            nc.scalar.dma_start(out[rows(tt), :], res[:])
+            if tt == 0:
+                results.append(late.tile([P, TILES, W], F32, name="res", offset=4096))
+            res = results[0][:, tt, :]
+            nc.scalar.activation(res, diff[:], ACT.Copy, scale=0.7)
+            nc.scalar.dma_start(out[rows(tt), :], res)
 
         gather_alpha(0, 0)
-        gather_alpha(0, 1)
-        gather_words(0, 0)
-        gather_words(0, 1)
-        gather_alpha(1, 0)
         exp_beta(0)
+        gather_alpha(0, 1)
         weave(0, 0)
-        gather_scales(0)
         gather_beta(0, 0)
-        gather_alpha(1, 1)
-        gather_words(1, 0)
         quantize(0, 0)
         weave(0, 1)
-        gather_words(1, 1)
-        quantize(0, 1)
-        exp_beta(1)
-        gather_scales(1)
-        gather_alpha(2, 0)
-        product(0, 0)
         gather_beta(0, 1)
-        weave(1, 0)
-        gather_beta(1, 0)
-        weave(1, 1)
-        product(0, 1)
-        gather_beta(1, 1)
-        quantize(1, 0)
-        multiply(0, 0)
-        quantize(1, 1)
-        product(1, 0)
+        quantize(0, 1)
+        gather_alpha(1, 0)
+        scalar_beta(1, 0)
+        join(1, 0)
+        gather_alpha(1, 1)
+        scalar_beta(1, 1)
+        join(1, 1)
+        gather_words(0, 0)
+        gather_scales(0)
+        gather_words(0, 1)
+        gather_scales(1)
+        gather_words(1, 0)
+        gather_words(1, 1)
+        gather_alpha(2, 0)
+        scalar_beta(2, 0)
+        join(2, 0)
         gather_alpha(2, 1)
-        exp_beta(2)
-        multiply(0, 1)
-        product(1, 1)
-        gather_beta(2, 0)
+        scalar_beta(2, 1)
+        join(2, 1)
         gather_alpha(3, 0)
-        multiply(1, 0)
-        gather_beta(2, 1)
-        exp_beta(3)
-        gather_alpha(3, 1)
-        multiply(1, 1)
+        weave(1, 0)
+        weave(1, 1)
+        quantize(1, 0)
+        quantize(1, 1)
+        product(0, 0)
+        product(0, 1)
+        product(1, 0)
+        product(1, 1)
         product(2, 0)
         product(2, 1)
-        gather_beta(3, 0)
         product(3, 0)
         product(3, 1)
+        exp_y(0, 0)
+        exp_y(0, 1)
+        exp_beta(3)
+        exp_y(1, 0)
+        exp_y(1, 1)
+        multiply(0, 0)
+        multiply(0, 1)
         add_groups(0)
-        gather_beta(3, 1)
+        gather_beta(3, 0)
+        exp_y(2, 0)
+        exp_y(2, 1)
+        exp_y(3, 0)
+        exp_y(3, 1)
+        keep_sums(0)
+        gather_alpha(3, 1)
+        log_sums(0, "bank4")
+        multiply(1, 0)
+        multiply(1, 1)
         add_groups(1)
         multiply(2, 0)
         multiply(2, 1)
-        multiply(3, 0)
-        multiply(3, 1)
-        log_sums(0, "bank3")
         add_groups(2)
-        log_sums(1, "bank2")
-        finish(0)
+        multiply(3, 0)
+        gather_beta(3, 1)
+        multiply(3, 1)
         add_groups(3)
-        finish(1)
+        keep_sums(1)
+        keep_sums(2)
+        log_sums(1, "bank5")
+        keep_sums(3)
         log_sums(2, "bank6")
-        finish(2)
         log_sums(3, "bank7")
+        finish(0)
+        finish(1)
+        finish(2)
         finish(3)

@@ -25,10 +25,13 @@ HALF = 512
 HALVES = S // HALF
 COLS = HALF // 16
 CHUNK = 256
-SCALAR_BETA = (1, 2)
-ALPHA_WINDOW = 2048
+SCALAR_WINDOW = 2048
+ALPHA_WINDOW = S + 16
 BETA_WINDOW = HALF + 16
 MG_WINDOW = 512
+FUSED = 1
+LAST = TILES - 1
+SCALE = 0.7
 
 
 def tile_picked_ybcjr_log_p_kernel(
@@ -41,6 +44,9 @@ def tile_picked_ybcjr_log_p_kernel(
         late = ctx.enter_context(tc.tile_pool(name="late", bufs=1))
         psum = ctx.enter_context(tc.psum_pool(name="psum", bufs=1))
 
+        def sbuf(shape, dtype, name, slot=None):
+            return keep.tile(shape, dtype, name=name, tag=slot or name, align_bytes=64)
+
         def load_list(name, src):
             tile = lists.tile(list(src.shape), U16, name=name)
             nc.sync.dma_start(tile[:], src)
@@ -52,31 +58,32 @@ def tile_picked_ybcjr_log_p_kernel(
         def piece(h):
             return slice(h * COLS, (h + 1) * COLS)
 
-        warm = keep.tile([P, 3], F32, name="warm")
+        def half(h):
+            return slice(h * HALF, (h + 1) * HALF)
+
+        warm = sbuf([P, 2], F32, "warm")
         nc.vector.memset(warm[:, 0:1], 0.0)
         nc.scalar.activation(warm[:, 1:2], warm[:, 0:1], ACT.Exp)
-        scale_table = keep.tile([P, T], U8, name="scale_table", align_bytes=64)
+        scale_table = sbuf([P, T], U8, "scale_table")
         nc.vector.memset(scale_table[:].bitcast(I32), 0)
-        alpha_win = [keep.tile([P, ALPHA_WINDOW], F32, name="alpha_win%d" % tt) for tt in range(TILES - 1)]
-        alpha_win.append(late.tile([P, ALPHA_WINDOW], F32, name="alpha_win3", offset=0))
-        beta_raw = [
-            keep.tile([P, ALPHA_WINDOW if tt in SCALAR_BETA else R], F32, name="beta_raw%d" % tt) for tt in range(TILES)
-        ]
-        beta_win = [keep.tile([P, BETA_WINDOW], F32, name="beta_win%d" % tt) for tt in range(TILES)]
-        mg_win = {}
-        ident = keep.tile([P, P], F32, name="ident")
+        ident = sbuf([P, P], F32, "ident")
         make_identity(nc, ident[:])
 
-        word_table = [keep.tile([P, T], I32, name="word_table%d" % o) for o in range(PASSES)]
-        h_raw = {}
+        alpha_sb, beta_sb, word_table, h_raw = {}, {}, {}, {}
 
         def load_alpha(tt):
-            nc.sync.dma_start(alpha_win[tt][:, :R], alpha[rows(tt), :])
+            alpha_sb[tt] = sbuf([P, R if tt == FUSED else SCALAR_WINDOW], F32, "alpha%d" % tt)
+            nc.sync.dma_start(alpha_sb[tt][:, :R], alpha[rows(tt), :])
 
         def load_beta(tt):
-            nc.sync.dma_start(beta_raw[tt][:, :R], beta[rows(tt), :])
+            if tt == LAST:
+                beta_sb[tt] = late.tile([P, SCALAR_WINDOW], F32, name="beta_last", offset=0)
+            else:
+                beta_sb[tt] = sbuf([P, R if tt == FUSED else SCALAR_WINDOW], F32, "beta%d" % tt)
+            nc.sync.dma_start(beta_sb[tt][:, :R], beta[rows(tt), :])
 
         def load_words(o):
+            word_table[o] = sbuf([P, T], I32, "word_table%d" % o)
             nc.sync.dma_start(word_table[o][:], x_words[o].rearrange("p n t -> p (n t)").bitcast(I32))
 
         def load_scales():
@@ -87,7 +94,7 @@ def tile_picked_ybcjr_log_p_kernel(
                 )
 
         def load_h(c, o):
-            h_raw[c, o] = keep.tile([P, PACK, CHUNK], F32, name="h_raw%d_%d" % (c, o))
+            h_raw[c, o] = sbuf([P, PACK, CHUNK], F32, "h_raw%d_%d" % (c, o))
             src = hT[o * K_PASS : (o + 1) * K_PASS, c * CHUNK : (c + 1) * CHUNK]
             nc.sync.dma_start(h_raw[c, o][:], src.rearrange("(p j) w -> p j w", j=PACK))
 
@@ -96,218 +103,217 @@ def tile_picked_ybcjr_log_p_kernel(
         load_h(0, 0)
         load_beta(0)
         en_l = load_list("en_l", en)
-        load_alpha(1)
-        load_beta(1)
         load_h(0, 1)
         offs_l = load_list("offs_l", offs)
+        load_alpha(2)
         load_words(0)
         load_scales()
-        load_alpha(2)
         load_beta(2)
-        load_alpha(3)
+        load_alpha(LAST)
+        load_beta(LAST)
+        load_alpha(FUSED)
+        load_beta(FUSED)
         load_words(1)
         load_h(1, 0)
         load_h(1, 1)
-        load_beta(3)
         one_l = load_list("one_l", one)
         zero_l = load_list("zero_l", zero)
-        prior_sb = keep.tile([P, TILES, W], F32, name="prior_sb")
-        nc.sync.dma_start(prior_sb[:], prior.rearrange("(n p) w -> p n w", p=P))
+        prior_sb = [sbuf([P, W], F32, "prior%d" % tt) for tt in range(TILES)]
+        for tt in range(TILES):
+            nc.sync.dma_start(prior_sb[tt][:], prior[rows(tt), :])
 
-        eb, ys, turns, results = {}, {}, {}, []
-        ea, ab, words, scales, h_bf, h_codes, h_scales, ey, q2, sums = {}, {}, {}, {}, {}, {}, {}, {}, {}, {}
+        ea, eb, ab, words, h_bf, h_codes, h_scales, ys, ey, ex = {}, {}, {}, {}, {}, {}, {}, {}, {}, {}
+        turned, sums, mg, low = {}, {}, {}, {}
 
-        def exp_beta(tt):
-            nc.scalar.activation(beta_win[tt][:, :R], beta_raw[tt][:, :R], ACT.Exp, scale=0.5)
+        def gather_alpha(tt, h, slot=None):
+            ea[tt, h] = sbuf([P, HALF], F32, "ea%d_%d" % (tt, h), slot)
+            nc.scalar.activation(ea[tt, h][:], alpha_sb[tt][:].indirect(st_l[:, piece(h)]), ACT.Exp, scale=0.5)
 
-        def gather_alpha(tt, h):
-            tag = "h_codes1_1" if (tt, h) == (3, 1) else "ea%d_%d" % (tt, h)
-            ea[tt, h] = keep.tile([P, HALF], F32, name="ea%d_%d" % (tt, h), tag=tag, align_bytes=64)
-            nc.scalar.activation(ea[tt, h][:], alpha_win[tt][:].indirect(st_l[:, piece(h)]), ACT.Exp, scale=0.5)
+        def gather_beta(tt, h, slot=None):
+            eb[tt, h] = sbuf([P, HALF], F32, "eb%d_%d" % (tt, h), slot)
+            nc.scalar.activation(eb[tt, h][:], beta_sb[tt][:].indirect(en_l[:, piece(h)]), ACT.Exp, scale=0.5)
 
-        def gather_beta(tt, h):
-            tag = "ab0_1" if (tt, h) == (3, 0) else "ab%d_%d" % (tt, h)
-            ab[tt, h] = keep.tile([P, HALF], F32, name="ab%d_%d" % (tt, h), tag=tag, align_bytes=64)
-            nc.vector.tensor_tensor(ab[tt, h][:], beta_win[tt][:].indirect(en_l[:, piece(h)]), ea[tt, h][:], ALU.mult)
+        def join(engine, tt, h, dst):
+            ab[tt, h] = dst
+            engine.tensor_tensor(dst, ea[tt, h][:], eb[tt, h][:], ALU.mult)
 
-        def scalar_beta(tt, h):
-            eb[tt, h] = keep.tile([P, HALF], F32, name="eb%d_%d" % (tt, h))
-            nc.scalar.activation(eb[tt, h][:], beta_raw[tt][:].indirect(en_l[:, piece(h)]), ACT.Exp, scale=0.5)
+        def states(tt):
+            both = sbuf([P, S], F32, "ab%d" % tt)
+            for h in range(HALVES):
+                gather_alpha(tt, h)
+                gather_beta(tt, h)
+                join(nc.gpsimd, tt, h, both[:, half(h)])
+            ab[tt] = both[:]
 
-        def join(tt, h):
-            ab[tt, h] = keep.tile([P, HALF], F32, name="ab%d_%d" % (tt, h))
-            nc.gpsimd.tensor_tensor(ab[tt, h][:], eb[tt, h][:], ea[tt, h][:], ALU.mult)
-
-        def gather_words(o, h):
-            words[o, h] = keep.tile([P, HALF], U32, name="words%d_%d" % (o, h), align_bytes=64)
-            nc.vector.tensor_copy(words[o, h][:], word_table[o][:].bitcast(U32).indirect(offs_l[:, piece(h)]))
-
-        def gather_scales(h):
-            scales[h] = keep.tile([P, HALF], U8, name="scales%d" % h, align_bytes=64)
-            nc.vector.tensor_copy(scales[h][:], scale_table[:].indirect(offs_l[:, piece(h)]))
+        def gather_words(o):
+            words[o] = sbuf([P, S], U32, "words%d" % o)
+            nc.vector.tensor_copy(words[o][:], word_table[o][:].bitcast(U32).indirect(offs_l[:]))
 
         def weave(c, o):
-            h_bf[c, o] = keep.tile([P, CHUNK, PACK], BF16, name="h_bf%d_%d" % (c, o), align_bytes=64)
+            if o == 0:
+                h_bf[c] = sbuf([P, PASSES, CHUNK, PACK], BF16, "h_bf%d" % c)
             nc.vector.tensor_copy(
-                h_bf[c, o][:].rearrange("p (w i) j -> p w j i", i=4),
+                h_bf[c][:, o].rearrange("p (w i) j -> p w j i", i=4),
                 h_raw[c, o][:].rearrange("p j (w i) -> p w j i", i=4),
             )
 
-        def quantize(c, o):
-            h_codes[c, o] = keep.tile([P, CHUNK], U32, name="h_codes%d_%d" % (c, o), align_bytes=64)
-            h_scales[c, o] = keep.tile([P, CHUNK], U8, name="h_scales%d_%d" % (c, o), align_bytes=64)
+        def quantize(c):
+            h_codes[c] = sbuf([P, PASSES * CHUNK], U32, "h_codes%d" % c)
+            h_scales[c] = sbuf([P, PASSES * CHUNK], U8, "h_scales%d" % c)
             nc.vector.quantize_mx(
-                out=h_codes[c, o][:].bitcast(FP8X4),
-                scales=h_scales[c, o][:],
-                in_=h_bf[c, o][:].rearrange("p w j -> p (w j)"),
+                out=h_codes[c][:].bitcast(FP8X4),
+                scales=h_scales[c][:],
+                in_=h_bf[c][:].rearrange("p o w j -> p (o w j)"),
             )
 
         def product(tt, h):
             c, first = divmod(tt * P, CHUNK)
-            cols = slice(first, first + P)
-            y = psum.tile([P, HALF], F32, name="y", tag="bank%d" % (2 * tt + h))
+            ys[tt, h] = psum.tile([P, HALF], F32, name="y", tag="bank%d" % (HALVES * tt + h))
             for o in range(PASSES):
+                cols = slice(o * CHUNK + first, o * CHUNK + first + P)
                 nc.tensor.matmul_mx(
-                    out=y[:],
-                    lhsT=h_codes[c, o][:, cols].bitcast(FP8X4),
-                    lhsT_scale=h_scales[c, o][:, cols],
-                    rhs=words[o, h][:].bitcast(FP8X4),
-                    rhs_scale=scales[h][4 * o : P, :],
+                    out=ys[tt, h][:],
+                    lhsT=h_codes[c][:, cols].bitcast(FP8X4),
+                    lhsT_scale=h_scales[c][:, cols],
+                    rhs=words[o][:, half(h)].bitcast(FP8X4),
+                    rhs_scale=scales[4 * o : P, half(h)],
                     start=(o == 0),
                     stop=(o == PASSES - 1),
                 )
-            ys[tt, h] = y
 
-        def exp_y(tt, h):
-            tag = "beta_raw2" if (tt, h) == (0, 0) else "ey%d_%d" % (tt, h)
-            ey[tt, h] = keep.tile([P, 2, HALF // 2], F32, name="ey%d_%d" % (tt, h), tag=tag)
-            nc.scalar.activation(ey[tt, h][:], ys[tt, h][:].rearrange("p (m e) -> p e m", e=2), ACT.Exp, scale=0.5)
+        def exp_y(tt):
+            ey[tt] = sbuf([P, 2, S // 2], F32, "ey%d" % tt)
+            for h in range(HALVES):
+                dst = ey[tt][:, :, h * HALF // 2 : (h + 1) * HALF // 2]
+                nc.scalar.activation(dst, ys[tt, h][:].rearrange("p (m e) -> p e m", e=2), ACT.Exp, scale=0.5)
 
-        def multiply(tt, h):
-            tag = "h_bf1_1" if (tt, h) == (0, 0) else "q2%d_%d" % (tt, h)
-            q2[tt, h] = keep.tile([P, 2, HALF // 2], F32, name="q2%d_%d" % (tt, h), tag=tag, align_bytes=64)
+        def multiply(dst, states_product, exp_product):
             nc.vector.tensor_tensor(
-                q2[tt, h][:].rearrange("p e (b i) -> p b e i", i=4),
-                ab[tt, h][:].rearrange("p (b i e) -> p b e i", i=4, e=2),
-                ey[tt, h][:].rearrange("p e (b i) -> p b e i", i=4),
+                dst.rearrange("p e (b i) -> p b e i", i=4),
+                states_product.rearrange("p (b i e) -> p b e i", i=4, e=2),
+                exp_product.rearrange("p e (b i) -> p b e i", i=4),
                 ALU.mult,
             )
 
+        def multiply_tile(tt, slot=None):
+            whole = sbuf([P, 2, S // 2], F32, "ex%d" % tt, slot)
+            multiply(whole[:], ab[tt], ey[tt][:])
+            for h in range(HALVES):
+                ex[tt, h] = whole[:, :, h * HALF // 2 : (h + 1) * HALF // 2]
+
         def add_groups(tt):
-            turned = psum.tile([P, HALVES, P], F32, name="turned", tag="bank%d" % ((tt - 1) % 4))
+            turned[tt] = psum.tile([P, HALVES, P], F32, name="turned", tag="bank%d" % tt)
             for h in range(HALVES):
                 for d in range(D):
+                    if tt == FUSED:
+                        member = ex[tt, h][:, d:HALF:D]
+                    else:
+                        member = ex[tt, h][:, d % 2, d // 2 : HALF // 2 : 2]
                     nc.tensor.matmul(
-                        turned[:, h, :],
-                        lhsT=q2[tt, h][:, d % 2, d // 2 : HALF // 2 : 2],
+                        turned[tt][:, h, :],
+                        lhsT=member,
                         rhs=ident[:],
                         is_transpose=True,
                         start=(d == 0),
                         stop=(d == D - 1),
                     )
-            turns[tt] = turned
 
         def keep_sums(tt):
             if tt == 0:
-                sums[tt] = keep.tile([P, HALVES, P], F32, name="sums0", tag="words1_1", align_bytes=64)
+                sums[tt] = sbuf([P, HALVES, P], F32, "sums0", "words1")
             else:
                 sums[tt] = late.tile([P, HALVES, P], F32, name="sums%d" % tt, offset=1024 * (1 + tt))
-            nc.scalar.copy(sums[tt][:], turns[tt][:])
+            nc.scalar.copy(sums[tt][:], turned[tt][:])
 
-        def log_sums(tt, bank):
-            back = psum.tile([P, W], F32, name="back", tag=bank)
+        def log_sums(tt):
+            back = psum.tile([P, W], F32, name="back", tag="bank%d" % (TILES + tt))
             for h in range(HALVES):
                 nc.tensor.transpose(back[:, h * P : (h + 1) * P], sums[tt][:, h, :], ident[:])
             if tt == 0:
-                mg_win[tt] = late.tile([P, MG_WINDOW], F32, name="mg_win0", offset=0)
+                mg[tt] = late.tile([P, MG_WINDOW], F32, name="mg0", offset=0)
             else:
-                mg_win[tt] = keep.tile([P, MG_WINDOW], F32, name="mg_win%d" % tt)
-            nc.scalar.activation(mg_win[tt][:, :W], back[:], ACT.Ln)
+                mg[tt] = sbuf([P, MG_WINDOW], F32, "mg%d" % tt)
+            nc.scalar.activation(mg[tt][:, :W], back[:], ACT.Ln)
+
+        def add_prior(tt, slot=None):
+            low[tt] = sbuf([P, W], F32, "low%d" % tt, slot)
+            nc.vector.tensor_tensor(low[tt][:], mg[tt][:].indirect(zero_l[:]), prior_sb[tt][:], ALU.add)
 
         def finish(tt):
-            low = keep.tile([P, W], F32, name="low%d" % tt)
-            nc.vector.tensor_tensor(low[:], mg_win[tt][:].indirect(zero_l[:]), prior_sb[:, tt, :], ALU.add)
-            diff = keep.tile([P, W], F32, name="diff%d" % tt)
-            nc.vector.tensor_tensor(diff[:], mg_win[tt][:].indirect(one_l[:]), low[:], ALU.subtract)
-            if tt == 0:
-                results.append(late.tile([P, TILES, W], F32, name="res", offset=4096))
-            res = results[0][:, tt, :]
-            nc.scalar.activation(res, diff[:], ACT.Copy, scale=0.7)
-            nc.scalar.dma_start(out[rows(tt), :], res)
+            nc.vector.tensor_tensor(diff[:, tt, :], mg[tt][:].indirect(one_l[:]), low[tt][:], ALU.subtract)
+            res = sbuf([P, W], F32, "res%d" % tt)
+            nc.scalar.activation(res[:], diff[:, tt, :], ACT.Copy, scale=SCALE)
+            nc.scalar.dma_start(out[rows(tt), :], res[:])
 
-        gather_alpha(0, 0)
-        exp_beta(0)
-        gather_alpha(0, 1)
         weave(0, 0)
-        gather_beta(0, 0)
-        quantize(0, 0)
         weave(0, 1)
-        gather_beta(0, 1)
-        quantize(0, 1)
-        gather_alpha(1, 0)
-        scalar_beta(1, 0)
-        join(1, 0)
-        gather_alpha(1, 1)
-        scalar_beta(1, 1)
-        join(1, 1)
-        gather_words(0, 0)
-        gather_scales(0)
-        gather_words(0, 1)
-        gather_scales(1)
-        gather_words(1, 0)
-        gather_words(1, 1)
-        gather_alpha(2, 0)
-        scalar_beta(2, 0)
-        join(2, 0)
-        gather_alpha(2, 1)
-        scalar_beta(2, 1)
-        join(2, 1)
-        gather_alpha(3, 0)
+        quantize(0)
+        states(0)
+        gather_words(0)
+        scales = sbuf([P, S], U8, "scales")
+        nc.vector.tensor_copy(scales[:], scale_table[:].indirect(offs_l[:]))
+        gather_words(1)
+        states(2)
+        gather_alpha(LAST, 0)
+        gather_beta(LAST, 0)
+        join(nc.gpsimd, LAST, 0, sbuf([P, HALF], F32, "ab_last0")[:])
+        alpha_win = sbuf([P, ALPHA_WINDOW], F32, "alpha_win")
+        nc.scalar.activation(alpha_win[:, :R], alpha_sb[FUSED][:], ACT.Exp, scale=0.5)
+        beta_win = sbuf([P, BETA_WINDOW], F32, "beta_win")
+        nc.scalar.activation(beta_win[:, :R], beta_sb[FUSED][:], ACT.Exp, scale=0.5)
         weave(1, 0)
         weave(1, 1)
-        quantize(1, 0)
-        quantize(1, 1)
-        product(0, 0)
-        product(0, 1)
-        product(1, 0)
-        product(1, 1)
-        product(2, 0)
-        product(2, 1)
-        product(3, 0)
-        product(3, 1)
-        exp_y(0, 0)
-        exp_y(0, 1)
-        exp_beta(3)
-        exp_y(1, 0)
-        exp_y(1, 1)
-        multiply(0, 0)
-        multiply(0, 1)
+        quantize(1)
+        for tt in (FUSED, 0, 2, LAST):
+            for h in range(HALVES):
+                product(tt, h)
+
+        ey[FUSED] = sbuf([P, S], F32, "ey_fused")
+        for h in range(HALVES):
+            nc.scalar.activation(ey[FUSED][:, half(h)], ys[FUSED, h][:], ACT.Exp, scale=0.5)
+        exp_y(0)
+        gather_alpha(LAST, 1, "h_codes0")
+        exp_y(2)
+        exp_y(LAST)
+
+        with_alpha = sbuf([P, S], F32, "with_alpha", "h_raw1_1")
+        nc.vector.tensor_tensor(with_alpha[:], alpha_win[:].indirect(st_l[:]), ey[FUSED][:], ALU.mult)
+        multiply_tile(0, "h_bf1")
         add_groups(0)
-        gather_beta(3, 0)
-        exp_y(2, 0)
-        exp_y(2, 1)
-        exp_y(3, 0)
-        exp_y(3, 1)
         keep_sums(0)
-        gather_alpha(3, 1)
-        log_sums(0, "bank4")
-        multiply(1, 0)
-        multiply(1, 1)
-        add_groups(1)
-        multiply(2, 0)
-        multiply(2, 1)
+        gather_beta(LAST, 1, "h_codes1")
+        log_sums(0)
+        for h in range(HALVES):
+            ex[FUSED, h] = sbuf([P, HALF], F32, "ex_fused%d" % h)[:]
+            nc.vector.tensor_tensor(ex[FUSED, h], beta_win[:].indirect(en_l[:, piece(h)]), with_alpha[:, half(h)], ALU.mult)
+        add_groups(FUSED)
+        multiply_tile(2)
         add_groups(2)
-        multiply(3, 0)
-        gather_beta(3, 1)
-        multiply(3, 1)
-        add_groups(3)
+        join(nc.vector, LAST, 1, sbuf([P, HALF], F32, "ab_last1")[:])
+        ex[LAST, 0] = late.tile([P, 2, HALF // 2], F32, name="ex_last0", offset=5120)[:]
+        ex[LAST, 1] = sbuf([P, 2, HALF // 2], F32, "ex_last1")[:]
+        for h in range(HALVES):
+            multiply(ex[LAST, h], ab[LAST, h], ey[LAST][:, :, h * HALF // 2 : (h + 1) * HALF // 2])
+        add_groups(LAST)
+
         keep_sums(1)
         keep_sums(2)
-        log_sums(1, "bank5")
-        keep_sums(3)
-        log_sums(2, "bank6")
-        log_sums(3, "bank7")
+        log_sums(1)
+        log_sums(2)
+        scaled_prior = late.tile([P, W], F32, name="scaled_prior", offset=7168)
+        nc.scalar.activation(scaled_prior[:], prior_sb[LAST][:], ACT.Copy, scale=SCALE)
+        keep_sums(LAST)
+        log_sums(LAST)
+        scaled_mg = sbuf([P, MG_WINDOW], F32, "scaled_mg")
+        nc.scalar.activation(scaled_mg[:, :W], mg[LAST][:, :W], ACT.Copy, scale=SCALE)
+        add_prior(0, "ab_last0")
+        add_prior(1)
+        add_prior(2)
+        diff = sbuf([P, TILES, W], F32, "diff", "ex_last1")
         finish(0)
         finish(1)
+        scaled_low = sbuf([P, W], F32, "scaled_low")
+        nc.vector.tensor_tensor(scaled_low[:], scaled_mg[:].indirect(zero_l[:]), scaled_prior[:], ALU.add)
         finish(2)
-        finish(3)
+        nc.vector.tensor_tensor(diff[:, LAST, :], scaled_mg[:].indirect(one_l[:]), scaled_low[:], ALU.subtract)
+        nc.sync.dma_start(out[rows(LAST), :], diff[:, LAST, :])

from contextlib import ExitStack

import concourse.mybir as mybir
from concourse.masks import make_identity

K, T, S, V, D, R, W = 1024, 2048, 1024, 512, 4, 256, 256
FLOPS = 2 * K * S * V

F32 = mybir.dt.float32
BF16 = mybir.dt.bfloat16
I32 = mybir.dt.int32
U32 = mybir.dt.uint32
U16 = mybir.dt.uint16
U8 = mybir.dt.uint8
FP8X4 = mybir.dt.float8_e4m3fn_x4
ACT = mybir.ActivationFunctionType
ALU = mybir.AluOpType

P = 128
PACK = 4
K_PASS = P * PACK
PASSES = K // K_PASS
TILES = V // P
HALF = 512
HALVES = S // HALF
COLS = HALF // 16
CHUNK = 256
SCALAR_WINDOW = 2048
ALPHA_WINDOW = S + 16
BETA_WINDOW = HALF + 16
MG_WINDOW = 512
FUSED = 1
LAST = TILES - 1
SCALE = 0.7


def tile_picked_ybcjr_log_p_kernel(
    tc, x_words, x_scales, hT, alpha, beta, prior, offs, st, en, one, zero, out
):
    nc = tc.nc
    with ExitStack() as ctx:
        lists = ctx.enter_context(tc.tile_pool(name="lists", bufs=1))
        keep = ctx.enter_context(tc.tile_pool(name="keep", bufs=1))
        late = ctx.enter_context(tc.tile_pool(name="late", bufs=1))
        psum = ctx.enter_context(tc.psum_pool(name="psum", bufs=1))

        def sbuf(shape, dtype, name, slot=None):
            return keep.tile(shape, dtype, name=name, tag=slot or name, align_bytes=64)

        def load_list(name, src):
            tile = lists.tile(list(src.shape), U16, name=name)
            nc.sync.dma_start(tile[:], src)
            return tile

        def rows(tt):
            return slice(tt * P, (tt + 1) * P)

        def piece(h):
            return slice(h * COLS, (h + 1) * COLS)

        def half(h):
            return slice(h * HALF, (h + 1) * HALF)

        warm = sbuf([P, 2], F32, "warm")
        nc.vector.memset(warm[:, 0:1], 0.0)
        nc.scalar.activation(warm[:, 1:2], warm[:, 0:1], ACT.Exp)
        scale_table = sbuf([P, T], U8, "scale_table")
        nc.vector.memset(scale_table[:].bitcast(I32), 0)
        ident = sbuf([P, P], F32, "ident")
        make_identity(nc, ident[:])

        alpha_sb, beta_sb, word_table, h_raw = {}, {}, {}, {}

        def load_alpha(tt):
            alpha_sb[tt] = sbuf([P, R if tt == FUSED else SCALAR_WINDOW], F32, "alpha%d" % tt)
            nc.sync.dma_start(alpha_sb[tt][:, :R], alpha[rows(tt), :])

        def load_beta(tt):
            if tt == LAST:
                beta_sb[tt] = late.tile([P, SCALAR_WINDOW], F32, name="beta_last", offset=0)
            else:
                beta_sb[tt] = sbuf([P, R if tt == FUSED else SCALAR_WINDOW], F32, "beta%d" % tt)
            nc.sync.dma_start(beta_sb[tt][:, :R], beta[rows(tt), :])

        def load_words(o):
            word_table[o] = sbuf([P, T], I32, "word_table%d" % o)
            nc.sync.dma_start(word_table[o][:], x_words[o].rearrange("p n t -> p (n t)").bitcast(I32))

        def load_scales():
            for q in range(4):
                nc.sync.dma_start(
                    scale_table[32 * q : 32 * q + 4 * PASSES, :].bitcast(I32),
                    x_scales[:, 4 * q : 4 * q + 4, :].bitcast(I32),
                )

        def load_h(c, o):
            h_raw[c, o] = sbuf([P, PACK, CHUNK], F32, "h_raw%d_%d" % (c, o))
            src = hT[o * K_PASS : (o + 1) * K_PASS, c * CHUNK : (c + 1) * CHUNK]
            nc.sync.dma_start(h_raw[c, o][:], src.rearrange("(p j) w -> p j w", j=PACK))

        st_l = load_list("st_l", st)
        load_alpha(0)
        load_h(0, 0)
        load_beta(0)
        en_l = load_list("en_l", en)
        load_h(0, 1)
        offs_l = load_list("offs_l", offs)
        load_alpha(2)
        load_words(0)
        load_scales()
        load_beta(2)
        load_alpha(LAST)
        load_beta(LAST)
        load_alpha(FUSED)
        load_beta(FUSED)
        load_words(1)
        load_h(1, 0)
        load_h(1, 1)
        one_l = load_list("one_l", one)
        zero_l = load_list("zero_l", zero)
        prior_sb = [sbuf([P, W], F32, "prior%d" % tt) for tt in range(TILES)]
        for tt in range(TILES):
            nc.sync.dma_start(prior_sb[tt][:], prior[rows(tt), :])

        ea, eb, ab, words, h_bf, h_codes, h_scales, ys, ey, ex = {}, {}, {}, {}, {}, {}, {}, {}, {}, {}
        turned, sums, mg, low = {}, {}, {}, {}

        def gather_alpha(tt, h, slot=None):
            ea[tt, h] = sbuf([P, HALF], F32, "ea%d_%d" % (tt, h), slot)
            nc.scalar.activation(ea[tt, h][:], alpha_sb[tt][:].indirect(st_l[:, piece(h)]), ACT.Exp, scale=0.5)

        def gather_beta(tt, h, slot=None):
            eb[tt, h] = sbuf([P, HALF], F32, "eb%d_%d" % (tt, h), slot)
            nc.scalar.activation(eb[tt, h][:], beta_sb[tt][:].indirect(en_l[:, piece(h)]), ACT.Exp, scale=0.5)

        def join(engine, tt, h, dst):
            ab[tt, h] = dst
            engine.tensor_tensor(dst, ea[tt, h][:], eb[tt, h][:], ALU.mult)

        def states(tt):
            both = sbuf([P, S], F32, "ab%d" % tt)
            for h in range(HALVES):
                gather_alpha(tt, h)
                gather_beta(tt, h)
                join(nc.gpsimd, tt, h, both[:, half(h)])
            ab[tt] = both[:]

        def gather_words(o):
            words[o] = sbuf([P, S], U32, "words%d" % o)
            nc.vector.tensor_copy(words[o][:], word_table[o][:].bitcast(U32).indirect(offs_l[:]))

        def weave(c, o):
            if o == 0:
                h_bf[c] = sbuf([P, PASSES, CHUNK, PACK], BF16, "h_bf%d" % c)
            nc.vector.tensor_copy(
                h_bf[c][:, o].rearrange("p (w i) j -> p w j i", i=4),
                h_raw[c, o][:].rearrange("p j (w i) -> p w j i", i=4),
            )

        def quantize(c):
            h_codes[c] = sbuf([P, PASSES * CHUNK], U32, "h_codes%d" % c)
            h_scales[c] = sbuf([P, PASSES * CHUNK], U8, "h_scales%d" % c)
            nc.vector.quantize_mx(
                out=h_codes[c][:].bitcast(FP8X4),
                scales=h_scales[c][:],
                in_=h_bf[c][:].rearrange("p o w j -> p (o w j)"),
            )

        def product(tt, h):
            c, first = divmod(tt * P, CHUNK)
            ys[tt, h] = psum.tile([P, HALF], F32, name="y", tag="bank%d" % (HALVES * tt + h))
            for o in range(PASSES):
                cols = slice(o * CHUNK + first, o * CHUNK + first + P)
                nc.tensor.matmul_mx(
                    out=ys[tt, h][:],
                    lhsT=h_codes[c][:, cols].bitcast(FP8X4),
                    lhsT_scale=h_scales[c][:, cols],
                    rhs=words[o][:, half(h)].bitcast(FP8X4),
                    rhs_scale=scales[4 * o : P, half(h)],
                    start=(o == 0),
                    stop=(o == PASSES - 1),
                )

        def exp_y(tt):
            ey[tt] = sbuf([P, 2, S // 2], F32, "ey%d" % tt)
            for h in range(HALVES):
                dst = ey[tt][:, :, h * HALF // 2 : (h + 1) * HALF // 2]
                nc.scalar.activation(dst, ys[tt, h][:].rearrange("p (m e) -> p e m", e=2), ACT.Exp, scale=0.5)

        def multiply(dst, states_product, exp_product):
            nc.vector.tensor_tensor(
                dst.rearrange("p e (b i) -> p b e i", i=4),
                states_product.rearrange("p (b i e) -> p b e i", i=4, e=2),
                exp_product.rearrange("p e (b i) -> p b e i", i=4),
                ALU.mult,
            )

        def multiply_tile(tt, slot=None):
            whole = sbuf([P, 2, S // 2], F32, "ex%d" % tt, slot)
            multiply(whole[:], ab[tt], ey[tt][:])
            for h in range(HALVES):
                ex[tt, h] = whole[:, :, h * HALF // 2 : (h + 1) * HALF // 2]

        def add_groups(tt):
            turned[tt] = psum.tile([P, HALVES, P], F32, name="turned", tag="bank%d" % tt)
            for h in range(HALVES):
                for d in range(D):
                    if tt == FUSED:
                        member = ex[tt, h][:, d:HALF:D]
                    else:
                        member = ex[tt, h][:, d % 2, d // 2 : HALF // 2 : 2]
                    nc.tensor.matmul(
                        turned[tt][:, h, :],
                        lhsT=member,
                        rhs=ident[:],
                        is_transpose=True,
                        start=(d == 0),
                        stop=(d == D - 1),
                    )

        def keep_sums(tt):
            if tt == 0:
                sums[tt] = sbuf([P, HALVES, P], F32, "sums0", "words1")
            else:
                sums[tt] = late.tile([P, HALVES, P], F32, name="sums%d" % tt, offset=1024 * (1 + tt))
            nc.scalar.copy(sums[tt][:], turned[tt][:])

        def log_sums(tt):
            back = psum.tile([P, W], F32, name="back", tag="bank%d" % (TILES + tt))
            for h in range(HALVES):
                nc.tensor.transpose(back[:, h * P : (h + 1) * P], sums[tt][:, h, :], ident[:])
            if tt == 0:
                mg[tt] = late.tile([P, MG_WINDOW], F32, name="mg0", offset=0)
            else:
                mg[tt] = sbuf([P, MG_WINDOW], F32, "mg%d" % tt)
            nc.scalar.activation(mg[tt][:, :W], back[:], ACT.Ln)

        def add_prior(tt, slot=None):
            low[tt] = sbuf([P, W], F32, "low%d" % tt, slot)
            nc.vector.tensor_tensor(low[tt][:], mg[tt][:].indirect(zero_l[:]), prior_sb[tt][:], ALU.add)

        def finish(tt):
            nc.vector.tensor_tensor(diff[:, tt, :], mg[tt][:].indirect(one_l[:]), low[tt][:], ALU.subtract)
            res = sbuf([P, W], F32, "res%d" % tt)
            nc.scalar.activation(res[:], diff[:, tt, :], ACT.Copy, scale=SCALE)
            nc.scalar.dma_start(out[rows(tt), :], res[:])

        weave(0, 0)
        weave(0, 1)
        quantize(0)
        states(0)
        gather_words(0)
        scales = sbuf([P, S], U8, "scales")
        nc.vector.tensor_copy(scales[:], scale_table[:].indirect(offs_l[:]))
        gather_words(1)
        states(2)
        gather_alpha(LAST, 0)
        gather_beta(LAST, 0)
        join(nc.gpsimd, LAST, 0, sbuf([P, HALF], F32, "ab_last0")[:])
        alpha_win = sbuf([P, ALPHA_WINDOW], F32, "alpha_win")
        nc.scalar.activation(alpha_win[:, :R], alpha_sb[FUSED][:], ACT.Exp, scale=0.5)
        beta_win = sbuf([P, BETA_WINDOW], F32, "beta_win")
        nc.scalar.activation(beta_win[:, :R], beta_sb[FUSED][:], ACT.Exp, scale=0.5)
        weave(1, 0)
        weave(1, 1)
        quantize(1)
        for tt in (FUSED, 0, 2, LAST):
            for h in range(HALVES):
                product(tt, h)

        ey[FUSED] = sbuf([P, S], F32, "ey_fused")
        for h in range(HALVES):
            nc.scalar.activation(ey[FUSED][:, half(h)], ys[FUSED, h][:], ACT.Exp, scale=0.5)
        exp_y(0)
        gather_alpha(LAST, 1, "h_codes0")
        exp_y(2)
        exp_y(LAST)

        with_alpha = sbuf([P, S], F32, "with_alpha", "h_raw1_1")
        nc.vector.tensor_tensor(with_alpha[:], alpha_win[:].indirect(st_l[:]), ey[FUSED][:], ALU.mult)
        multiply_tile(0, "h_bf1")
        add_groups(0)
        keep_sums(0)
        gather_beta(LAST, 1, "h_codes1")
        log_sums(0)
        for h in range(HALVES):
            ex[FUSED, h] = sbuf([P, HALF], F32, "ex_fused%d" % h)[:]
            nc.vector.tensor_tensor(ex[FUSED, h], beta_win[:].indirect(en_l[:, piece(h)]), with_alpha[:, half(h)], ALU.mult)
        add_groups(FUSED)
        multiply_tile(2)
        add_groups(2)
        join(nc.vector, LAST, 1, sbuf([P, HALF], F32, "ab_last1")[:])
        ex[LAST, 0] = late.tile([P, 2, HALF // 2], F32, name="ex_last0", offset=5120)[:]
        ex[LAST, 1] = sbuf([P, 2, HALF // 2], F32, "ex_last1")[:]
        for h in range(HALVES):
            multiply(ex[LAST, h], ab[LAST, h], ey[LAST][:, :, h * HALF // 2 : (h + 1) * HALF // 2])
        add_groups(LAST)

        keep_sums(1)
        keep_sums(2)
        log_sums(1)
        log_sums(2)
        scaled_prior = late.tile([P, W], F32, name="scaled_prior", offset=7168)
        nc.scalar.activation(scaled_prior[:], prior_sb[LAST][:], ACT.Copy, scale=SCALE)
        keep_sums(LAST)
        log_sums(LAST)
        scaled_mg = sbuf([P, MG_WINDOW], F32, "scaled_mg")
        nc.scalar.activation(scaled_mg[:, :W], mg[LAST][:, :W], ACT.Copy, scale=SCALE)
        add_prior(0, "ab_last0")
        add_prior(1)
        add_prior(2)
        diff = sbuf([P, TILES, W], F32, "diff", "ex_last1")
        finish(0)
        finish(1)
        scaled_low = sbuf([P, W], F32, "scaled_low")
        nc.vector.tensor_tensor(scaled_low[:], scaled_mg[:].indirect(zero_l[:]), scaled_prior[:], ALU.add)
        finish(2)
        nc.vector.tensor_tensor(diff[:, LAST, :], scaled_mg[:].indirect(one_l[:]), scaled_low[:], ALU.subtract)
        nc.sync.dma_start(out[rows(LAST), :], diff[:, LAST, :])
